import numpy as np
import ml_dtypes


def mxq(x, axis, fmt="e4m3"):
    dtype, down = {"e4m3": (ml_dtypes.float8_e4m3fn, 7), "e5m2": (ml_dtypes.float8_e5m2, 14)}[fmt]
    v = np.moveaxis(np.asarray(x, np.float32).astype(ml_dtypes.bfloat16).astype(np.float64), axis, -1)
    blocks = v.reshape(v.shape[:-1] + (-1, 32))
    amax = np.abs(blocks).max(-1, keepdims=True)
    byte = np.maximum(np.where(amax > 0, np.frexp(amax)[1] - 1 + 127, 0) - down, 1)
    scale = np.exp2(byte - 127.0)
    codes = (blocks / scale).astype(np.float32).astype(dtype).astype(np.float64)
    return np.moveaxis((codes * scale).reshape(v.shape), -1, axis)


WIDE = False


def mx_kscale(k):
    if not WIDE:
        return np.ones(k)
    levels = np.array([10, -10, 5, -5, 0])
    if k % 512:
        return np.exp2(np.random.permutation(np.resize(levels, k // 32))).repeat(32)
    a = np.empty((k // 512, 16))
    for p in range(k // 512):
        a[p, :8] = np.random.permutation(np.resize(levels, 8))
        for g in range(8):
            far = levels[np.abs(levels - a[p, g]) >= 10]
            a[p, g + 8] = far[np.random.randint(len(far))]
    return np.exp2(a.ravel()).repeat(32)


def f64(x):
    return np.asarray(x).astype(np.float64)


def striped(idx):
    return np.tile(idx.reshape(-1, 16).T, (8, 1)).astype(np.uint16)


def unstriped(offs):
    return offs[:16].T.reshape(-1).astype(np.int64)


def relu2(v):
    return np.maximum(v, 0.0) ** 2


K, T, E, C, H, N = 1536, 1280, 6, 128, 512, 128


def by_expert(wq, xq):
    return np.concatenate([wq[e].T @ xq[:, e * C:(e + 1) * C] for e in range(E)], axis=1)


def setup_inputs():
    n = np.random.standard_normal
    s = mx_kscale(K)[:, None]
    u = mx_kscale(H)
    return {
        "xT": (n((K, T)) * s).astype(np.float32),
        "xr": n((N, T)).astype(np.float32),
        "w1": (n((E, K, H)) / np.sqrt(K) / s[None] * u[None, None, :]).astype(np.float32),
        "w2": (n((E, H, N)) / np.sqrt(H) / u[None, :, None] ** 2).astype(np.float32),
        "gate": np.tile(np.random.uniform(0.2, 1.0, E * C), (N, 1)).astype(np.float32),
        "offs": striped(np.random.permutation(T)[:E * C]),
    }


def reference(xT, xr, w1, w2, gate, offs):
    idx = unstriped(offs)
    xq = mxq(f64(xT)[:, idx], 0, "e4m3")
    h = relu2(by_expert(mxq(f64(w1), 1, "e4m3"), xq))
    y = by_expert(mxq(f64(w2), 1, "e4m3"), mxq(h, 0, "e4m3"))
    out = f64(xr).copy()
    out[:, idx] += f64(gate) * y
    return out

from contextlib import ExitStack

import concourse.mybir as mybir

K, T, E, C, H, N = 1536, 1280, 6, 128, 512, 128
S = E * C
FLOPS = 2 * S * (K * H + H * N)

F32 = mybir.dt.float32
BF16 = mybir.dt.bfloat16
U32 = mybir.dt.uint32
U16 = mybir.dt.uint16
U8 = mybir.dt.uint8
FP8X4 = mybir.dt.float8_e4m3fn_x4
COPY = mybir.ActivationFunctionType.Copy
RELU = mybir.ActivationFunctionType.Relu
SQUARE = mybir.ActivationFunctionType.Square
MULT = mybir.AluOpType.mult
ADD = mybir.AluOpType.add

P = 128
PACK = 4
K_PASS = P * PACK
PASSES = K // K_PASS
TILES = H // P

X_SCALAR = 512
W_VECTOR = 56
X_CHUNKS = ((512, 1024), (1024, 1280), (0, 512))
W2_CHUNKS = {("w2", 0, 5): ((0, 512), (512, 640)), ("w2", 5, 6): ((640, 768),)}
SCATTERS = {1: (0, 256), 3: (256, 448), 4: (448, 608), 5: (608, 768)}
AHEAD = 6
OUT_PIECES = ((0, 448), (448, 832), (832, 1088), (1088, 1280))


def tile_moe_res_mlp_relu2_kernel(tc, xT, xr, w1, w2, gate, offs, out):
    nc = tc.nc
    with ExitStack() as ctx:
        held = ctx.enter_context(tc.tile_pool(name="held", bufs=1))
        xraws = ctx.enter_context(tc.tile_pool(name="xraws", bufs=3))
        wraws = ctx.enter_context(tc.tile_pool(name="wraws", bufs=6))
        xgrps = ctx.enter_context(tc.tile_pool(name="xgrps", bufs=2))
        wgrps = ctx.enter_context(tc.tile_pool(name="wgrps", bufs=3))
        wcods = ctx.enter_context(tc.tile_pool(name="wcods", bufs=6))
        hids = ctx.enter_context(tc.tile_pool(name="hids", bufs=2))
        psum = ctx.enter_context(tc.psum_pool(name="psum", bufs=1))
        ypsum = ctx.enter_context(tc.psum_pool(name="ypsum", bufs=2))

        lists = held.tile([P, S // 16], U16, name="lists")
        planes = held.tile([P, T], U8, name="planes", align_bytes=64)
        nc.gpsimd.memset(planes[:], 0)
        window = held.tile([P, T], F32, name="window")
        nc.gpsimd.memset(window[:], 0.0)

        words = [held.tile([P, T], U32, name=f"words{s}", align_bytes=64) for s in range(PASSES)]
        slot_words = [held.tile([P, S], U32, name=f"slot_words{s}", align_bytes=64) for s in range(PASSES)]
        slot_planes = held.tile([P, S], U8, name="slot_planes", align_bytes=64)
        w2_grp = held.tile([P, E * N * PACK], BF16, name="w2_grp", align_bytes=64)
        w2_codes = held.tile([P, E * N], U32, name="w2_codes", align_bytes=64)
        w2_scales = held.tile([P, E * N], U8, name="w2_scales", align_bytes=64)
        gates = held.tile([P, S], F32, name="gates")
        y_all = held.tile([P, S], F32, name="y_all")
        result = held.tile([P, T], F32, name="result")

        raw, grp, codes, scales, acc, relu, hid, y_sum = {}, {}, {}, {}, {}, {}, {}, {}

        def load(item):
            kind = item[0]
            queue = nc.scalar if kind == "w" and item[1] > 1 and sum(item[1:]) % 2 == 0 else nc.sync
            if kind == "x":
                s = item[1]
                t = xraws.tile([P, PACK, T], F32, name="x_raw")
                queue.dma_start(out=t[:], in_=xT[s * K_PASS : (s + 1) * K_PASS, :].rearrange("(p j) t -> p j t", j=PACK))
                raw[item] = t
                if s == 0:
                    nc.sync.dma_start(lists[:], offs)
            elif kind == "w":
                e, s = item[1], item[2]
                t = wraws.tile([P, PACK * H], F32, name="w_raw")
                queue.dma_start(out=t[:], in_=w1[e, s * K_PASS : (s + 1) * K_PASS, :].rearrange("(p j) i -> p (j i)", j=PACK))
                raw[item] = t
            elif kind == "w2":
                a, b = item[1:]
                if a:
                    t = wraws.tile([P, b - a, PACK * N], F32, name="w_raw")
                else:
                    t = held.tile([P, b - a, PACK * N], F32, name="w2_raw")
                raw[item] = t
                queue.dma_start(out=t[:], in_=w2[a:b].rearrange("e (p j) n -> p e (j n)", j=PACK))
            elif kind == "gate":
                queue.dma_start(out=gates[:], in_=gate)
            else:
                t = wraws.tile([P, T], F32, name="w_raw")
                raw[item] = t
                queue.dma_start(out=t[:], in_=xr)

        def cast(item):
            kind = item[0]
            if kind == "x":
                g = xgrps.tile([P, T, PACK], BF16, name="x_grp", align_bytes=64)
                grp[item] = g
                dst = g[:].rearrange("p (c i) t -> p c t i", i=4)
                src = raw[item][:].rearrange("p t (c i) -> p c t i", i=4)
                nc.scalar.activation(dst[:, : X_SCALAR // 4], src[:, : X_SCALAR // 4], COPY)
                nc.vector.tensor_copy(dst[:, X_SCALAR // 4 :], src[:, X_SCALAR // 4 :])
            elif kind == "w":
                g = wgrps.tile([P, H * PACK], BF16, name="w_grp", align_bytes=64)
                grp[item] = g
                dst = g[:].rearrange("p (t m j) -> p m j t", t=TILES, j=PACK)
                src = raw[item][:].rearrange("p (j m t) -> p m j t", t=TILES, j=PACK)
                cut = (88 if item[1:] == (E - 1, PASSES - 1) else W_VECTOR) if item[1] else 128 * (item[2] == 0)
                if cut:
                    nc.vector.tensor_copy(dst[:, :cut], src[:, :cut])
                if cut < 128:
                    nc.scalar.activation(dst[:, cut:], src[:, cut:], COPY)
            elif kind == "w2":
                a, b = item[1:]
                for e in range(a, b):
                    dst = w2_grp[:, e * N * PACK : (e + 1) * N * PACK].rearrange("p (c i j) -> p c j i", i=4, j=PACK)
                    src = raw[item][:, e - a, :].rearrange("p (j c i) -> p c j i", i=4, j=PACK)
                    nc.scalar.activation(dst, src, COPY)

        def quantise(item):
            kind = item[0]
            if kind == "x":
                s = item[1]
                flat = grp[item][:].rearrange("p n t -> p (n t)")
                for a, b in X_CHUNKS:
                    nc.vector.quantize_mx(
                        out=words[s][:, a:b].bitcast(FP8X4),
                        scales=planes[4 * s : P, a:b],
                        in_=flat[:, PACK * a : PACK * b],
                    )
            elif kind == "w":
                c = wcods.tile([P, H], U32, name="w_codes", align_bytes=64)
                z = wcods.tile([P, H], U8, name="w_scales", align_bytes=64)
                width = P if item[1:] == (E - 1, PASSES - 1) else H
                for a in range(0, H, width):
                    b = a + width
                    nc.vector.quantize_mx(out=c[:, a:b].bitcast(FP8X4), scales=z[:, a:b], in_=grp[item][:, PACK * a : PACK * b])
                codes[item], scales[item] = c, z
            elif kind == "w2":
                for a, b in W2_CHUNKS[item]:
                    nc.vector.quantize_mx(
                        out=w2_codes[:, a:b].bitcast(FP8X4),
                        scales=w2_scales[:, a:b],
                        in_=w2_grp[:, PACK * a : PACK * b],
                    )

        def gather(s):
            nc.vector.tensor_copy(slot_words[s][:], words[s][:].indirect(lists[:]))
            if s == PASSES - 1:
                nc.vector.tensor_copy(slot_planes[:], planes[:].indirect(lists[:]))

        def multiply(e, s):
            if e < E - 1:
                if s < PASSES - 1:
                    return
                sums = psum.tile([P, TILES, C], F32, name="sums", bufs=2)
                acc[e] = [sums[:, t, :] for t in range(TILES)]
                whole[e] = sums
                order = [(t, k) for t in range(TILES) for k in range(PASSES)]
            else:
                if s == 0:
                    tiles = [psum.tile([P, C], F32, name=f"last{t}") for t in range(TILES)]
                    acc[e] = [tile[:] for tile in tiles]
                order = [(t, s) for t in range(TILES)]
            cols = slice(e * C, (e + 1) * C)
            for t, k in order:
                rows = slice(t * P, (t + 1) * P)
                nc.tensor.matmul_mx(
                    out=acc[e][t],
                    lhsT=codes["w", e, k][:, rows].bitcast(FP8X4),
                    lhsT_scale=scales["w", e, k][:, rows],
                    rhs=slot_words[k][:, cols].bitcast(FP8X4),
                    rhs_scale=slot_planes[4 * k : P, cols],
                    start=(k == 0),
                    stop=(k == PASSES - 1),
                )

        def rectify(e):
            r = hids.tile([P, TILES, C], F32, name="relu_out")
            if e < E - 1:
                nc.scalar.activation(r[:], whole[e][:], RELU)
            else:
                for t in range(TILES):
                    if t % 2:
                        nc.vector.tensor_scalar_max(r[:, t, :], acc[e][t], 0.0)
                    else:
                        nc.scalar.activation(r[:, t, :], acc[e][t], RELU)
            relu[e] = r

        def square(e):
            g = hids.tile([P, C, TILES], BF16, name="h_grp", align_bytes=64)
            src = relu[e][:].rearrange("p t c -> p c t")
            half = C // 2
            nc.scalar.activation(g[:, :half, :], src[:, :half, :], SQUARE)
            nc.vector.tensor_tensor(g[:, half:, :], src[:, half:, :], src[:, half:, :], MULT)
            hid[e] = g

        def second(e):
            c = hids.tile([P, C], U32, name="h_codes", align_bytes=64)
            z = hids.tile([P, C], U8, name="h_scales", align_bytes=64)
            nc.vector.quantize_mx(out=c[:].bitcast(FP8X4), scales=z[:], in_=hid[e][:].rearrange("p c t -> p (c t)"))
            y = ypsum.tile([P, C], F32, name="y")
            cols = slice(e * N, (e + 1) * N)
            nc.tensor.matmul_mx(
                out=y[:],
                lhsT=w2_codes[:, cols].bitcast(FP8X4),
                lhsT_scale=w2_scales[:, cols],
                rhs=c[:].bitcast(FP8X4),
                rhs_scale=z[:],
                start=True,
                stop=True,
            )
            y_sum[e] = y

        def collect(e):
            if e < E - 1:
                nc.scalar.activation(y_all[:, e * C : (e + 1) * C], y_sum[e][:], COPY)
            else:
                nc.vector.tensor_copy(y_all[:, e * C : (e + 1) * C], y_sum[e][:])

        def scatter(e):
            if e in SCATTERS:
                a, b = SCATTERS[e]
                nc.vector.tensor_tensor(window[:].indirect(lists[:, a // 16 : b // 16]), y_all[:, a:b], gates[:, a:b], MULT)

        whole = {}
        due = {}
        items = []
        items += [("w", 0, 0), ("x", 0), ("w2", 0, E - 1), ("x", 1), ("w", 0, 1), ("x", 2), ("w", 0, 2), ("gate",)]
        items += [("w", e, s) for e in range(1, E) for s in range(PASSES)]
        items += [("w2", E - 1, E), ("xr",)]

        for item in items[:AHEAD]:
            load(item)
        waiting = []
        stages = ((5, scatter), (4, collect), (3, second), (2, square), (1, rectify))
        for i in range(len(items) + 6):
            if i + AHEAD < len(items):
                load(items[i + AHEAD])
            for delay, stage in stages:
                for e in range(E):
                    if due.get(e) == i - delay:
                        stage(e)
            if 0 <= i - 1 < len(items):
                item = items[i - 1]
                quantise(item)
                if item[0] == "x":
                    gather(item[1])
                if item[0] == "w":
                    waiting.append(item)
                if i > items.index(("x", PASSES - 1)):
                    for w in waiting:
                        multiply(w[1], w[2])
                        if w[2] == PASSES - 1:
                            due[w[1]] = i
                    waiting = []
            if i < len(items):
                cast(items[i])

        for a, b in OUT_PIECES:
            nc.vector.tensor_tensor(result[:, a:b], window[:, a:b], raw["xr",][:, a:b], ADD)
            nc.sync.dma_start(out=out[:, a:b], in_=result[:, a:b])
